import numpy as np
import ml_dtypes


def mxq(x, axis, fmt="e4m3"):
    dtype, down = {"e4m3": (ml_dtypes.float8_e4m3fn, 7), "e5m2": (ml_dtypes.float8_e5m2, 14)}[fmt]
    v = np.moveaxis(np.asarray(x, np.float32).astype(ml_dtypes.bfloat16).astype(np.float64), axis, -1)
    blocks = v.reshape(v.shape[:-1] + (-1, 32))
    amax = np.abs(blocks).max(-1, keepdims=True)
    byte = np.maximum(np.where(amax > 0, np.frexp(amax)[1] - 1 + 127, 0) - down, 1)
    scale = np.exp2(byte - 127.0)
    codes = (blocks / scale).astype(np.float32).astype(dtype).astype(np.float64)
    return np.moveaxis((codes * scale).reshape(v.shape), -1, axis)


WIDE = False


def mx_kscale(k):
    if not WIDE:
        return np.ones(k)
    levels = np.array([10, -10, 5, -5, 0])
    if k % 512:
        return np.exp2(np.random.permutation(np.resize(levels, k // 32))).repeat(32)
    a = np.empty((k // 512, 16))
    for p in range(k // 512):
        a[p, :8] = np.random.permutation(np.resize(levels, 8))
        for g in range(8):
            far = levels[np.abs(levels - a[p, g]) >= 10]
            a[p, g + 8] = far[np.random.randint(len(far))]
    return np.exp2(a.ravel()).repeat(32)


def f64(x):
    return np.asarray(x).astype(np.float64)


def striped(idx):
    return np.tile(np.asarray(idx).reshape(-1, 16).T, (8, 1)).astype(np.uint16)


def unstriped(offs):
    return offs[:16].T.reshape(-1).astype(np.int64)


E2M1 = np.array([0.0, 0.5, 1.0, 1.5, 2.0, 3.0, 4.0, 6.0, -0.0, -0.5, -1.0, -1.5, -2.0, -3.0, -4.0, -6.0])


def pack_weight(w, fmt):
    k, n = w.shape
    w = f64(np.asarray(w, np.float32).astype(ml_dtypes.bfloat16)).reshape(k // 32, 32, n)
    amax = np.abs(w).max(1)
    if fmt == "e4m3":
        byte = np.frexp(amax)[1] - 1 + 127 - 7
    else:
        mant, ex = np.frexp(amax / 6.0)
        byte = np.where(mant > 0.5, ex, ex - 1) + 127
    byte = np.clip(np.where(amax > 0, byte, 1), 1, 254)
    scaled = (w * np.exp2(127.0 - byte)[:, None, :]).reshape(k, n).astype(np.float32)
    by_word = np.ascontiguousarray(scaled.reshape(k // 512, 128, 4, n).transpose(0, 1, 3, 2))
    if fmt == "e4m3":
        words = by_word.astype(ml_dtypes.float8_e4m3fn).view(np.uint8)
    else:
        c = by_word.astype(ml_dtypes.float4_e2m1fn).view(np.uint8) & 0xF
        words = (c[..., 0::2] | (c[..., 1::2] << 4)).reshape(k // 512, 128, 2 * n)
    return np.ascontiguousarray(words), np.ascontiguousarray(byte.astype(np.uint8).reshape(k // 512, 16, n))


def unpack_weight(words, scales, fmt):
    g, _, n = scales.shape
    words = np.ascontiguousarray(words).reshape(g, 128, n, -1)
    if fmt == "e4m3":
        vals = words.view(ml_dtypes.float8_e4m3fn).astype(np.float64)
    else:
        nib = np.empty((g, 128, n, 4), np.uint8)
        nib[..., 0::2] = words & 0xF
        nib[..., 1::2] = words >> 4
        vals = E2M1[nib]
    vals = vals * np.repeat(np.exp2(scales.astype(np.float64) - 127.0), 8, axis=1)[..., None]
    return vals.transpose(0, 1, 3, 2).reshape(g * 512, n)


def bf(x):
    return np.asarray(x, np.float32).astype(ml_dtypes.bfloat16)


def planes(Y):
    r, m = Y.shape
    b = f64(bf(Y)).reshape(r // 32, 32, m)
    amax = np.abs(b).max(1)
    byte = np.clip(np.where(amax > 0, np.frexp(amax)[1] - 1 + 127 - 7, 1), 1, 254)
    codes = (b * np.exp2(127.0 - byte)[:, None, :]).reshape(r, m).astype(np.float32).astype(ml_dtypes.float8_e4m3fn).view(np.uint8)
    words = codes.reshape(r // 512, 128, 4, m).transpose(0, 1, 3, 2)
    return np.ascontiguousarray(words), np.ascontiguousarray(byte.astype(np.uint8).reshape(r // 512, 16, m))


D, T, I, M = 512, 2048, 512, 512


def setup_inputs():
    n = np.random.standard_normal
    idx = np.random.permutation(T)[:I]
    fd = mx_kscale(D)
    ptsp = pack_weight(n((D, T)) / fd[:, None], "e4m3")
    return {
        "pts_words": ptsp[0],
        "pts_scales": ptsp[1],
        "cent": (n((D, M)) * 0.2 / np.sqrt(D) * fd[:, None]).astype(np.float32),
        "pn": (np.random.uniform(1.0, 2.0, (I, 1))).astype(np.float32),
        "cn": (np.random.uniform(1.0, 2.0, (1, M))).astype(np.float32),
        "offs": striped(idx),
    }


def reference(pts_words, pts_scales, cent, pn, cn, offs):
    idx = unstriped(offs)
    ptsu = unpack_weight(pts_words, pts_scales, "e4m3")
    ptsidxg = ptsu[:, idx]
    centq = mxq(f64(cent), 0, "e4m3")
    a = ptsidxg.T @ centq
    r = 1.0 / (1.0 + f64(pn) + f64(cn) - 2.0 * a)
    s = r / np.sum(r, axis=1, keepdims=True)
    st = s.T
    x = np.square(st) / np.sum(st, axis=1, keepdims=True)
    xt = x.T
    y = xt / np.sum(xt, axis=1, keepdims=True) * 512.0
    words, scales = planes(y)
    return y, words, scales

@@ -1,0 +1,210 @@
+from contextlib import ExitStack
+
+import concourse.mybir as mybir
+from concourse.masks import make_identity
+
+D, T, I, M = 512, 2048, 512, 512
+FLOPS = 2 * D * I * M
+
+F32 = mybir.dt.float32
+BF16 = mybir.dt.bfloat16
+I32 = mybir.dt.int32
+U32 = mybir.dt.uint32
+U16 = mybir.dt.uint16
+U8 = mybir.dt.uint8
+FP8X4 = mybir.dt.float8_e4m3fn_x4
+ALU = mybir.AluOpType
+ACT = mybir.ActivationFunctionType
+AX = mybir.AxisListType
+
+P = 128
+PACK = 4
+HALF = M // 2
+
+
+def interleave(engine_copy, dst, src):
+    engine_copy(out=dst.rearrange("p (c i) t -> p c t i", i=4), in_=src.rearrange("p t (c i) -> p c t i", i=4))
+
+
+def tile_attend_dectarget_pl_kernel(tc, pts_words, pts_scales, cent, pn, cn, offs, out_0, out_1, out_2):
+    nc = tc.nc
+    with ExitStack() as ctx:
+        held = ctx.enter_context(tc.tile_pool(name="held", bufs=1))
+        psum = ctx.enter_context(tc.psum_pool(name="psum", bufs=1))
+
+        offsets = held.tile([P, I // 16], U16, name="offsets")
+        pool_words = held.tile([P, T], U32, name="pool_words", align_bytes=64)
+        pool_scales = held.tile([P, T], U8, name="pool_scales", align_bytes=64)
+        pn4 = held.tile([P, PACK], F32, name="pn4")
+        cn4 = held.tile([P, PACK], F32, name="cn4")
+        warm = held.tile([P, 1], F32, name="warm")
+        warm_out = held.tile([P, 1], F32, name="warm_out")
+        ident = held.tile([P, P], F32, name="ident", align_bytes=64)
+
+        nc.vector.memset(pool_scales[:].bitcast(I32), 0)
+        nc.vector.memset(warm[:], 1.0)
+        nc.sync.dma_start(offsets[:], offs)
+        nc.scalar.dma_start(cn4[:], cn.rearrange("o (p j) -> p (o j)", j=PACK))
+        nc.sync.dma_start(pool_words[:].bitcast(I32), pts_words[0].rearrange("p c r -> p (c r)").bitcast(I32))
+        nc.scalar.dma_start(pn4[:], pn.rearrange("(p t) o -> p (t o)", t=PACK))
+        for q in range(4):
+            nc.scalar.dma_start(pool_scales[32 * q : 32 * q + 4, :].bitcast(I32), pts_scales[0, 4 * q : 4 * q + 4, :].bitcast(I32))
+        nc.scalar.activation(warm_out[:], warm[:], ACT.Abs_reciprocal_sqrt)
+        cent_rows = cent.rearrange("(p j) m -> p j m", j=PACK)
+        cent_raw = []
+        for h in range(2):
+            raw = held.tile([P, PACK, HALF], F32, name="cent_raw%d" % h)
+            nc.sync.dma_start(raw[:], cent_rows[:, :, h * HALF : (h + 1) * HALF])
+            cent_raw.append(raw)
+        make_identity(nc, ident[:])
+
+        pn1 = held.tile([P, PACK], F32, name="pn1")
+        pn1_neg = held.tile([P, PACK], F32, name="pn1_neg")
+        nc.gpsimd.tensor_scalar(pn1[:], pn4[:], 1.0, 1.0, ALU.mult, ALU.add)
+        nc.gpsimd.tensor_scalar(pn1_neg[:], pn4[:], -1.0, -1.0, ALU.mult, ALU.add)
+
+        cn_bank = psum.tile([P, PACK, P], F32, name="cn_bank")
+        for j in range(PACK):
+            nc.tensor.transpose(cn_bank[:, j, :], cn4[:, j : j + 1].to_broadcast([P, P]), ident[:])
+        cn_rows = held.tile([P, P, PACK], F32, name="cn_rows")
+        nc.scalar.copy(out=cn_rows[:], in_=cn_bank[:].rearrange("q j p -> q p j"))
+        cn_all = cn_rows[:].rearrange("q p j -> q (p j)")
+
+        got_scales = held.tile([P, I], U8, name="got_scales", tag="gathered", align_bytes=64)
+        pt_scales = held.tile([P, PACK, P], U8, name="pt_scales", align_bytes=64)
+        nc.vector.tensor_copy(got_scales[:], pool_scales[:].indirect(offsets[:]))
+        nc.vector.tensor_copy(
+            out=pt_scales[:].rearrange("p r (c i) -> p c r i", i=16),
+            in_=got_scales[:].rearrange("p (c i r) -> p c r i", i=16, r=PACK),
+        )
+        got_words = held.tile([P, I], U32, name="got_words", tag="gathered", align_bytes=64)
+        pt_words = held.tile([P, PACK, P], U32, name="pt_words", align_bytes=64)
+        nc.vector.tensor_copy(got_words[:], pool_words[:].indirect(offsets[:]))
+        nc.vector.tensor_copy(
+            out=pt_words[:].bitcast(I32).rearrange("p r (c i) -> p c r i", i=4),
+            in_=got_words[:].bitcast(I32).rearrange("p (c i r) -> p c r i", i=4, r=PACK),
+        )
+
+        cent_words = held.tile([P, M], U32, name="cent_words", align_bytes=64)
+        cent_scales = held.tile([P, M], U8, name="cent_scales", align_bytes=64)
+        for h, engine_copy in enumerate((nc.scalar.copy, nc.vector.tensor_copy)):
+            cols = slice(h * HALF, (h + 1) * HALF)
+            grouped = held.tile([P, HALF, PACK], BF16, name="cent_bf%d" % h, align_bytes=64)
+            interleave(engine_copy, grouped[:], cent_raw[h][:])
+            nc.vector.quantize_mx(
+                out=cent_words[:, cols].bitcast(FP8X4),
+                scales=cent_scales[:, cols],
+                in_=grouped[:].rearrange("p m j -> p (m j)"),
+            )
+
+        a = []
+        for t in range(PACK):
+            bank = psum.tile([P, M], F32, name="a%d" % t)
+            nc.tensor.matmul_mx(
+                out=bank[:],
+                lhsT=pt_words[:, t, :].bitcast(FP8X4),
+                lhsT_scale=pt_scales[:, t, :],
+                rhs=cent_words[:].bitcast(FP8X4),
+                rhs_scale=cent_scales[:],
+                start=True,
+                stop=True,
+            )
+            a.append(bank)
+
+        def tiles(name):
+            return [held.tile([P, M], F32, name="%s%d" % (name, t)) for t in range(PACK)]
+
+        z, u, q_abs, sign, r, s, s2, x = (tiles(n) for n in ("z", "u", "q", "sign", "r", "s", "s2", "x"))
+        r_sum = held.tile([P, PACK], F32, name="r_sum")
+        r_inv = held.tile([P, PACK], F32, name="r_inv")
+        f_banks = [psum.tile([P, 2, P], F32, name="f_bank%d" % h) for h in range(2)]
+
+        def distance(t):
+            nc.vector.scalar_tensor_tensor(z[t][:], a[t][:], -2.0, cn_all, ALU.mult, ALU.add)
+            nc.scalar.activation(u[t][:], z[t][:], ACT.Abs_reciprocal_sqrt, bias=pn1[:, t : t + 1])
+            nc.scalar.activation(q_abs[t][:], u[t][:], ACT.Square)
+
+        def half_sign(t):
+            nc.vector.tensor_scalar(sign[t][:], z[t][:], pn1_neg[:, t : t + 1], 0.5, ALU.is_ge, ALU.subtract)
+
+        def kernel_values(t):
+            col = slice(t, t + 1)
+            nc.vector.scalar_tensor_tensor(r[t][:], q_abs[t][:], 1.0, sign[t][:], ALU.mult, ALU.mult, accum_out=r_sum[:, col])
+            nc.vector.reciprocal(r_inv[:, col], r_sum[:, col])
+
+        def assignments(t):
+            col = slice(t, t + 1)
+            if t < PACK - 1:
+                nc.scalar.activation(s[t][:], r[t][:], ACT.Copy, scale=r_inv[:, col])
+            for j in range(PACK):
+                if t == PACK - 1 and j % 2 == 0:
+                    cols = slice(j * P, (j + 2) * P)
+                    nc.vector.tensor_scalar(s[t][:, cols], r[t][:, cols], r_inv[:, col], None, ALU.mult)
+                nc.tensor.matmul(
+                    f_banks[j // 2][:, j % 2, :],
+                    lhsT=s[t][:, j * P : (j + 1) * P],
+                    rhs=ident[:],
+                    is_transpose=True,
+                    start=(t == 0 and j % 2 == 0),
+                    stop=(t == PACK - 1 and j % 2 == 1),
+                )
+
+        distance(0)
+        distance(1)
+        half_sign(0)
+        for t in range(PACK):
+            kernel_values(t)
+            if t + 2 < PACK:
+                distance(t + 2)
+            if t + 1 < PACK:
+                half_sign(t + 1)
+        for t in range(PACK):
+            assignments(t)
+        for t in range(PACK):
+            nc.scalar.activation(s2[t][:], r[t][:], ACT.Square, scale=r_inv[:, t : t + 1])
+
+        f_sum = held.tile([P, PACK], F32, name="f_sum")
+        f_inv = held.tile([P, PACK], F32, name="f_inv")
+        g_bank = psum.tile([P, M], F32, name="g_bank")
+        for h in range(2):
+            pair = slice(2 * h, 2 * h + 2)
+            nc.vector.tensor_reduce(f_sum[:, pair], f_banks[h][:], AX.X, ALU.add)
+            nc.vector.reciprocal(f_inv[:, pair], f_sum[:, pair])
+            for j in range(2 * h, 2 * h + 2):
+                nc.tensor.transpose(g_bank[:, j * P : (j + 1) * P], f_inv[:, j : j + 1].to_broadcast([P, P]), ident[:])
+
+        x_sum = held.tile([P, PACK], F32, name="x_sum")
+        x_inv = held.tile([P, PACK], F32, name="x_inv")
+        y_scale = held.tile([P, PACK], F32, name="y_scale")
+        y = held.tile([P, PACK, M], F32, name="y")
+        out_rows = out_0.rearrange("(p t) m -> p t m", t=PACK)
+        for t in range(PACK):
+            col = slice(t, t + 1)
+            nc.vector.scalar_tensor_tensor(x[t][:], s2[t][:], 1.0, g_bank[:], ALU.mult, ALU.mult, accum_out=x_sum[:, col])
+            nc.vector.reciprocal(x_inv[:, col], x_sum[:, col])
+            if t == PACK - 1:
+                nc.vector.tensor_scalar(y[:, t, :], x[t][:], x_inv[:, col], float(M), ALU.mult, ALU.mult)
+            else:
+                nc.vector.tensor_scalar(y_scale[:, col], x_inv[:, col], float(M), None, ALU.mult)
+                nc.scalar.activation(y[:, t, :], x[t][:], ACT.Copy, scale=y_scale[:, col])
+            nc.sync.dma_start(out_rows[:, t, :], y[:, t, :])
+
+        y_words = held.tile([P, M], U32, name="y_words", align_bytes=64)
+        y_scales = held.tile([P, M], U8, name="y_scales", align_bytes=64)
+        words_out = out_1[0].rearrange("p c r -> p (c r)").bitcast(I32)
+        shares = ((0, HALF, nc.vector.tensor_copy), (HALF, P, nc.scalar.copy), (HALF + P, P, nc.scalar.copy))
+        for first, width, engine_copy in shares:
+            cols = slice(first, first + width)
+            grouped = held.tile([P, width, PACK], BF16, name="y_bf%d" % first, align_bytes=64)
+            interleave(engine_copy, grouped[:], y[:, :, cols])
+            nc.vector.quantize_mx(
+                out=y_words[:, cols].bitcast(FP8X4),
+                scales=y_scales[:, cols],
+                in_=grouped[:].rearrange("p m t -> p (m t)"),
+            )
+            if first != HALF:
+                stored = slice(0, HALF) if first == 0 else slice(HALF, M)
+                nc.sync.dma_start(words_out[:, stored], y_words[:, stored].bitcast(I32))
+        for q in range(4):
+            queue = nc.sync if q % 2 == 0 else nc.scalar
+            queue.dma_start(out_2[0, 4 * q : 4 * q + 4, :].bitcast(I32), y_scales[32 * q : 32 * q + 4, :].bitcast(I32))

@@ -1,7 +1,6 @@
 from contextlib import ExitStack
 
 import concourse.mybir as mybir
-from concourse.masks import make_identity
 
 D, T, I, M = 512, 2048, 512, 512
 FLOPS = 2 * D * I * M
@@ -34,29 +33,30 @@ def tile_attend_dectarget_pl_kernel(tc, pts_words, pts_scales, cent, pn, cn, off
 
         offsets = held.tile([P, I // 16], U16, name="offsets")
         pool_words = held.tile([P, T], U32, name="pool_words", align_bytes=64)
-        pool_scales = held.tile([P, T], U8, name="pool_scales", align_bytes=64)
+        pool_scales = held.tile([P, T], U8, name="pool_scales", tag="scales_slot", align_bytes=64)
         pn4 = held.tile([P, PACK], F32, name="pn4")
-        cn4 = held.tile([P, PACK], F32, name="cn4")
+        cn4 = held.tile([P, PACK], F32, name="cn4", tag="second_half_slot")
         warm = held.tile([P, 1], F32, name="warm")
         warm_out = held.tile([P, 1], F32, name="warm_out")
+        zeros = held.tile([P, P], F32, name="zeros", tag="first_half_slot")
         ident = held.tile([P, P], F32, name="ident", align_bytes=64)
 
         nc.vector.memset(pool_scales[:].bitcast(I32), 0)
         nc.vector.memset(warm[:], 1.0)
+        nc.gpsimd.memset(zeros[:], 0.0)
+        nc.gpsimd.affine_select(
+            out=ident[:], in_=zeros[:], pattern=[[-1, P]], compare_op=ALU.not_equal, fill=1.0, base=0, channel_multiplier=1
+        )
         nc.sync.dma_start(offsets[:], offs)
         nc.scalar.dma_start(cn4[:], cn.rearrange("o (p j) -> p (o j)", j=PACK))
         nc.sync.dma_start(pool_words[:].bitcast(I32), pts_words[0].rearrange("p c r -> p (c r)").bitcast(I32))
         nc.scalar.dma_start(pn4[:], pn.rearrange("(p t) o -> p (t o)", t=PACK))
         for q in range(4):
             nc.scalar.dma_start(pool_scales[32 * q : 32 * q + 4, :].bitcast(I32), pts_scales[0, 4 * q : 4 * q + 4, :].bitcast(I32))
-        nc.scalar.activation(warm_out[:], warm[:], ACT.Abs_reciprocal_sqrt)
         cent_rows = cent.rearrange("(p j) m -> p j m", j=PACK)
-        cent_raw = []
-        for h in range(2):
-            raw = held.tile([P, PACK, HALF], F32, name="cent_raw%d" % h)
-            nc.sync.dma_start(raw[:], cent_rows[:, :, h * HALF : (h + 1) * HALF])
-            cent_raw.append(raw)
-        make_identity(nc, ident[:])
+        cent_raw0 = held.tile([P, PACK, HALF], F32, name="cent_raw0", tag="first_half_slot")
+        nc.sync.dma_start(cent_raw0[:], cent_rows[:, :, :HALF])
+        nc.scalar.activation(warm_out[:], warm[:], ACT.Abs_reciprocal_sqrt)
 
         pn1 = held.tile([P, PACK], F32, name="pn1")
         pn1_neg = held.tile([P, PACK], F32, name="pn1_neg")
@@ -66,70 +66,98 @@ def tile_attend_dectarget_pl_kernel(tc, pts_words, pts_scales, cent, pn, cn, off
         cn_bank = psum.tile([P, PACK, P], F32, name="cn_bank")
         for j in range(PACK):
             nc.tensor.transpose(cn_bank[:, j, :], cn4[:, j : j + 1].to_broadcast([P, P]), ident[:])
+        cent_raw1 = held.tile([P, PACK, HALF], F32, name="cent_raw1", tag="second_half_slot")
+        nc.sync.dma_start(cent_raw1[:], cent_rows[:, :, HALF:])
         cn_rows = held.tile([P, P, PACK], F32, name="cn_rows")
         nc.scalar.copy(out=cn_rows[:], in_=cn_bank[:].rearrange("q j p -> q p j"))
         cn_all = cn_rows[:].rearrange("q p j -> q (p j)")
 
-        got_scales = held.tile([P, I], U8, name="got_scales", tag="gathered", align_bytes=64)
+        got_scales = held.tile([P, I], U8, name="got_scales", align_bytes=64)
         pt_scales = held.tile([P, PACK, P], U8, name="pt_scales", align_bytes=64)
         nc.vector.tensor_copy(got_scales[:], pool_scales[:].indirect(offsets[:]))
         nc.vector.tensor_copy(
             out=pt_scales[:].rearrange("p r (c i) -> p c r i", i=16),
             in_=got_scales[:].rearrange("p (c i r) -> p c r i", i=16, r=PACK),
         )
-        got_words = held.tile([P, I], U32, name="got_words", tag="gathered", align_bytes=64)
-        pt_words = held.tile([P, PACK, P], U32, name="pt_words", align_bytes=64)
-        nc.vector.tensor_copy(got_words[:], pool_words[:].indirect(offsets[:]))
-        nc.vector.tensor_copy(
-            out=pt_words[:].bitcast(I32).rearrange("p r (c i) -> p c r i", i=4),
-            in_=got_words[:].bitcast(I32).rearrange("p (c i r) -> p c r i", i=4, r=PACK),
-        )
-
         cent_words = held.tile([P, M], U32, name="cent_words", align_bytes=64)
         cent_scales = held.tile([P, M], U8, name="cent_scales", align_bytes=64)
-        for h, engine_copy in enumerate((nc.scalar.copy, nc.vector.tensor_copy)):
+
+        def quantise_centres(h, raw):
             cols = slice(h * HALF, (h + 1) * HALF)
-            grouped = held.tile([P, HALF, PACK], BF16, name="cent_bf%d" % h, align_bytes=64)
-            interleave(engine_copy, grouped[:], cent_raw[h][:])
+            cent_bf = held.tile([P, HALF, PACK], BF16, name="cent_bf%d" % h, align_bytes=64)
+            interleave(nc.scalar.copy, cent_bf[:], raw[:])
             nc.vector.quantize_mx(
-                out=cent_words[:, cols].bitcast(FP8X4),
-                scales=cent_scales[:, cols],
-                in_=grouped[:].rearrange("p m j -> p (m j)"),
+                out=cent_words[:, cols].bitcast(FP8X4), scales=cent_scales[:, cols], in_=cent_bf[:].rearrange("p m j -> p (m j)")
             )
 
-        a = []
-        for t in range(PACK):
-            bank = psum.tile([P, M], F32, name="a%d" % t)
+        got_words = held.tile([P, I], U32, name="got_words", tag="scales_slot", align_bytes=64)
+        pt_words = held.tile([P, PACK, P], U32, name="pt_words", align_bytes=64)
+        nc.vector.tensor_copy(got_words[:], pool_words[:].indirect(offsets[:]))
+        for pair in (slice(0, 2), slice(2, 4)):
+            nc.vector.tensor_copy(
+                out=pt_words[:, pair, :].bitcast(I32).rearrange("p r (c i) -> p c r i", i=4),
+                in_=got_words[:].bitcast(I32).rearrange("p (c i r) -> p c r i", i=4, r=PACK)[:, :, pair, :],
+            )
+        quantise_centres(0, cent_raw0)
+        quantise_centres(1, cent_raw1)
+
+        def product(out, t, cols):
             nc.tensor.matmul_mx(
-                out=bank[:],
+                out=out,
                 lhsT=pt_words[:, t, :].bitcast(FP8X4),
                 lhsT_scale=pt_scales[:, t, :],
-                rhs=cent_words[:].bitcast(FP8X4),
-                rhs_scale=cent_scales[:],
+                rhs=cent_words[:, cols].bitcast(FP8X4),
+                rhs_scale=cent_scales[:, cols],
                 start=True,
                 stop=True,
             )
-            a.append(bank)
+
+        a_half = [psum.tile([P, 2, HALF], F32, name="a_half%d" % h, tag="a%d" % h) for h in range(2)]
+        for h in range(2):
+            for t in range(2):
+                product(a_half[h][:, t, :], t, slice(h * HALF, (h + 1) * HALF))
+        a_whole = [psum.tile([P, M], F32, name="a_whole%d" % t) for t in range(2, PACK)]
+        for t in range(2, PACK):
+            product(a_whole[t - 2][:], t, slice(0, M))
 
         def tiles(name):
             return [held.tile([P, M], F32, name="%s%d" % (name, t)) for t in range(PACK)]
 
-        z, u, q_abs, sign, r, s, s2, x = (tiles(n) for n in ("z", "u", "q", "sign", "r", "s", "s2", "x"))
+        def quarters(name):
+            return [held.tile([P, 2, 2, HALF], F32, name="%s%d" % (name, k)) for k in range(2)]
+
+        def row(pair, t):
+            return pair[0][:, :, t, :] if t < 2 else pair[1][:, t - 2, :, :]
+
+        def halves(ap):
+            return ap.rearrange("p (h c) -> p h c", h=2)
+
+        z, u, q_abs = (quarters(n) for n in ("z", "u", "q"))
+        sign, r, s, s2, x = (tiles(n) for n in ("sign", "r", "s", "s2", "x"))
         r_sum = held.tile([P, PACK], F32, name="r_sum")
         r_inv = held.tile([P, PACK], F32, name="r_inv")
         f_banks = [psum.tile([P, 2, P], F32, name="f_bank%d" % h) for h in range(2)]
 
-        def distance(t):
-            nc.vector.scalar_tensor_tensor(z[t][:], a[t][:], -2.0, cn_all, ALU.mult, ALU.add)
-            nc.scalar.activation(u[t][:], z[t][:], ACT.Abs_reciprocal_sqrt, bias=pn1[:, t : t + 1])
-            nc.scalar.activation(q_abs[t][:], u[t][:], ACT.Square)
+        def distance_half(h):
+            cn_twice = cn_all[:, h * HALF : (h + 1) * HALF].unsqueeze(1).to_broadcast([P, 2, HALF])
+            nc.vector.scalar_tensor_tensor(z[0][:, h, :, :], a_half[h][:], -2.0, cn_twice, ALU.mult, ALU.add)
+            for t in range(2):
+                nc.scalar.activation(u[0][:, h, t, :], z[0][:, h, t, :], ACT.Abs_reciprocal_sqrt, bias=pn1[:, t : t + 1])
+            nc.scalar.activation(q_abs[0][:, h, :, :], u[0][:, h, :, :], ACT.Square)
 
-        def half_sign(t):
-            nc.vector.tensor_scalar(sign[t][:], z[t][:], pn1_neg[:, t : t + 1], 0.5, ALU.is_ge, ALU.subtract)
+        def distance_whole(t):
+            nc.vector.scalar_tensor_tensor(row(z, t), halves(a_whole[t - 2][:]), -2.0, halves(cn_all), ALU.mult, ALU.add)
+            nc.scalar.activation(row(u, t), row(z, t), ACT.Abs_reciprocal_sqrt, bias=pn1[:, t : t + 1])
+            nc.scalar.activation(row(q_abs, t), row(u, t), ACT.Square)
+
+        def half_sign(t, hs):
+            nc.vector.tensor_scalar(halves(sign[t][:])[:, hs, :], row(z, t)[:, hs, :], pn1_neg[:, t : t + 1], 0.5, ALU.is_ge, ALU.subtract)
 
         def kernel_values(t):
             col = slice(t, t + 1)
-            nc.vector.scalar_tensor_tensor(r[t][:], q_abs[t][:], 1.0, sign[t][:], ALU.mult, ALU.mult, accum_out=r_sum[:, col])
+            nc.vector.scalar_tensor_tensor(
+                halves(r[t][:]), row(q_abs, t), 1.0, halves(sign[t][:]), ALU.mult, ALU.mult, accum_out=r_sum[:, col]
+            )
             nc.vector.reciprocal(r_inv[:, col], r_sum[:, col])
 
         def assignments(t):
@@ -149,15 +177,17 @@ def tile_attend_dectarget_pl_kernel(tc, pts_words, pts_scales, cent, pn, cn, off
                     stop=(t == PACK - 1 and j % 2 == 1),
                 )
 
-        distance(0)
-        distance(1)
-        half_sign(0)
+        for h in range(2):
+            distance_half(h)
+        for t in range(2, PACK):
+            distance_whole(t)
+        for h in range(2):
+            for t in range(2):
+                half_sign(t, slice(h, h + 1))
         for t in range(PACK):
+            if t >= 2:
+                half_sign(t, slice(0, 2))
             kernel_values(t)
-            if t + 2 < PACK:
-                distance(t + 2)
-            if t + 1 < PACK:
-                half_sign(t + 1)
         for t in range(PACK):
             assignments(t)
         for t in range(PACK):
@@ -165,46 +195,56 @@ def tile_attend_dectarget_pl_kernel(tc, pts_words, pts_scales, cent, pn, cn, off
 
         f_sum = held.tile([P, PACK], F32, name="f_sum")
         f_inv = held.tile([P, PACK], F32, name="f_inv")
-        g_bank = psum.tile([P, M], F32, name="g_bank")
+        g_banks = [psum.tile([P, HALF], F32, name="g_bank%d" % h, tag="a%d" % h) for h in range(2)]
+        g_whole = psum.tile([P, M], F32, name="g_whole")
         for h in range(2):
             pair = slice(2 * h, 2 * h + 2)
             nc.vector.tensor_reduce(f_sum[:, pair], f_banks[h][:], AX.X, ALU.add)
             nc.vector.reciprocal(f_inv[:, pair], f_sum[:, pair])
-            for j in range(2 * h, 2 * h + 2):
-                nc.tensor.transpose(g_bank[:, j * P : (j + 1) * P], f_inv[:, j : j + 1].to_broadcast([P, P]), ident[:])
+            for j in range(2):
+                nc.tensor.transpose(g_banks[h][:, j * P : (j + 1) * P], f_inv[:, 2 * h + j : 2 * h + j + 1].to_broadcast([P, P]), ident[:])
+        for j in range(PACK):
+            nc.tensor.transpose(g_whole[:, j * P : (j + 1) * P], f_inv[:, j : j + 1].to_broadcast([P, P]), ident[:])
 
+        x_part = held.tile([P, 2, 2], F32, name="x_part")
         x_sum = held.tile([P, PACK], F32, name="x_sum")
         x_inv = held.tile([P, PACK], F32, name="x_inv")
-        y_scale = held.tile([P, PACK], F32, name="y_scale")
         y = held.tile([P, PACK, M], F32, name="y")
         out_rows = out_0.rearrange("(p t) m -> p t m", t=PACK)
-        for t in range(PACK):
+        for h in range(2):
+            cols = slice(h * HALF, (h + 1) * HALF)
+            for t in range(2):
+                nc.vector.scalar_tensor_tensor(
+                    x[t][:, cols], s2[t][:, cols], 1.0, g_banks[h][:], ALU.mult, ALU.mult, accum_out=x_part[:, h, t : t + 1]
+                )
+        for t in range(2):
             col = slice(t, t + 1)
-            nc.vector.scalar_tensor_tensor(x[t][:], s2[t][:], 1.0, g_bank[:], ALU.mult, ALU.mult, accum_out=x_sum[:, col])
+            nc.vector.tensor_scalar(x_sum[:, col], x_part[:, 0, col], x_part[:, 1, col], 1.0 / M, ALU.add, ALU.mult)
             nc.vector.reciprocal(x_inv[:, col], x_sum[:, col])
-            if t == PACK - 1:
-                nc.vector.tensor_scalar(y[:, t, :], x[t][:], x_inv[:, col], float(M), ALU.mult, ALU.mult)
-            else:
-                nc.vector.tensor_scalar(y_scale[:, col], x_inv[:, col], float(M), None, ALU.mult)
-                nc.scalar.activation(y[:, t, :], x[t][:], ACT.Copy, scale=y_scale[:, col])
+            nc.scalar.activation(y[:, t, :], x[t][:], ACT.Copy, scale=x_inv[:, col])
             nc.sync.dma_start(out_rows[:, t, :], y[:, t, :])
+        for t in range(2, PACK):
+            nc.vector.scalar_tensor_tensor(x[t][:], s2[t][:], 1.0, g_whole[:], ALU.mult, ALU.mult, accum_out=x_sum[:, t : t + 1])
+        nc.vector.reciprocal(x_inv[:, 2:4], x_sum[:, 2:4])
+        for cols in (slice(HALF, M), slice(0, HALF)):
+            for t in range(2, PACK):
+                nc.vector.tensor_scalar(y[:, t, cols], x[t][:, cols], x_inv[:, t : t + 1], float(M), ALU.mult, ALU.mult)
+        nc.sync.dma_start(out_rows[:, 2:4, :], y[:, 2:4, :])
 
+        y_bf = held.tile([P, M, PACK], BF16, name="y_bf", align_bytes=64)
         y_words = held.tile([P, M], U32, name="y_words", align_bytes=64)
         y_scales = held.tile([P, M], U8, name="y_scales", align_bytes=64)
         words_out = out_1[0].rearrange("p c r -> p (c r)").bitcast(I32)
-        shares = ((0, HALF, nc.vector.tensor_copy), (HALF, P, nc.scalar.copy), (HALF + P, P, nc.scalar.copy))
-        for first, width, engine_copy in shares:
-            cols = slice(first, first + width)
-            grouped = held.tile([P, width, PACK], BF16, name="y_bf%d" % first, align_bytes=64)
-            interleave(engine_copy, grouped[:], y[:, :, cols])
+        for cols, engine_copy in ((slice(HALF, M), nc.scalar.copy), (slice(0, HALF), nc.vector.tensor_copy)):
+            interleave(engine_copy, y_bf[:, cols, :], y[:, :, cols])
+        for h in range(2):
+            cols = slice(h * HALF, (h + 1) * HALF)
             nc.vector.quantize_mx(
                 out=y_words[:, cols].bitcast(FP8X4),
                 scales=y_scales[:, cols],
-                in_=grouped[:].rearrange("p m t -> p (m t)"),
+                in_=y_bf[:, cols, :].rearrange("p m t -> p (m t)"),
             )
-            if first != HALF:
-                stored = slice(0, HALF) if first == 0 else slice(HALF, M)
-                nc.sync.dma_start(words_out[:, stored], y_words[:, stored].bitcast(I32))
+            nc.sync.dma_start(words_out[:, cols], y_words[:, cols].bitcast(I32))
         for q in range(4):
             queue = nc.sync if q % 2 == 0 else nc.scalar
             queue.dma_start(out_2[0, 4 * q : 4 * q + 4, :].bitcast(I32), y_scales[32 * q : 32 * q + 4, :].bitcast(I32))

@@ -19,6 +19,7 @@ AX = mybir.AxisListType
 P = 128
 PACK = 4
 HALF = M // 2
+HALF_BYTES = PACK * HALF * 4
 
 
 def interleave(engine_copy, dst, src):
@@ -29,16 +30,15 @@ def tile_attend_dectarget_pl_kernel(tc, pts_words, pts_scales, cent, pn, cn, off
     nc = tc.nc
     with ExitStack() as ctx:
         held = ctx.enter_context(tc.tile_pool(name="held", bufs=1))
+        late = ctx.enter_context(tc.tile_pool(name="late", bufs=1))
         psum = ctx.enter_context(tc.psum_pool(name="psum", bufs=1))
 
         offsets = held.tile([P, I // 16], U16, name="offsets")
-        pool_words = held.tile([P, T], U32, name="pool_words", align_bytes=64)
         pool_scales = held.tile([P, T], U8, name="pool_scales", tag="scales_slot", align_bytes=64)
-        pn4 = held.tile([P, PACK], F32, name="pn4")
-        cn4 = held.tile([P, PACK], F32, name="cn4", tag="second_half_slot")
+        cn4 = held.tile([P, PACK], F32, name="cn4", tag="lengths_slot")
         warm = held.tile([P, 1], F32, name="warm")
         warm_out = held.tile([P, 1], F32, name="warm_out")
-        zeros = held.tile([P, P], F32, name="zeros", tag="first_half_slot")
+        zeros = late.tile([P, P], F32, name="zeros", offset=HALF_BYTES - 256, align_bytes=64)
         ident = held.tile([P, P], F32, name="ident", align_bytes=64)
 
         nc.vector.memset(pool_scales[:].bitcast(I32), 0)
@@ -47,39 +47,41 @@ def tile_attend_dectarget_pl_kernel(tc, pts_words, pts_scales, cent, pn, cn, off
         nc.gpsimd.affine_select(
             out=ident[:], in_=zeros[:], pattern=[[-1, P]], compare_op=ALU.not_equal, fill=1.0, base=0, channel_multiplier=1
         )
+        cent_rows = cent.rearrange("(p j) m -> p j m", j=PACK)
+        cent_raw0 = held.tile([P, PACK, HALF], F32, name="cent_raw0")
         nc.sync.dma_start(offsets[:], offs)
         nc.scalar.dma_start(cn4[:], cn.rearrange("o (p j) -> p (o j)", j=PACK))
-        nc.sync.dma_start(pool_words[:].bitcast(I32), pts_words[0].rearrange("p c r -> p (c r)").bitcast(I32))
-        nc.scalar.dma_start(pn4[:], pn.rearrange("(p t) o -> p (t o)", t=PACK))
-        for q in range(4):
-            nc.scalar.dma_start(pool_scales[32 * q : 32 * q + 4, :].bitcast(I32), pts_scales[0, 4 * q : 4 * q + 4, :].bitcast(I32))
-        cent_rows = cent.rearrange("(p j) m -> p j m", j=PACK)
-        cent_raw0 = held.tile([P, PACK, HALF], F32, name="cent_raw0", tag="first_half_slot")
         nc.sync.dma_start(cent_raw0[:], cent_rows[:, :, :HALF])
+        for q in range(4):
+            nc.sync.dma_start(pool_scales[32 * q : 32 * q + 4, :].bitcast(I32), pts_scales[0, 4 * q : 4 * q + 4, :].bitcast(I32))
+        pool_words = late.tile([P, T], U32, name="pool_words", offset=HALF_BYTES, align_bytes=64)
+        nc.sync.dma_start(pool_words[:].bitcast(I32), pts_words[0].rearrange("p c r -> p (c r)").bitcast(I32))
+        cent_raw1 = late.tile([P, PACK, HALF], F32, name="cent_raw1", offset=0, align_bytes=64)
+        nc.sync.dma_start(cent_raw1[:], cent_rows[:, :, HALF:])
         nc.scalar.activation(warm_out[:], warm[:], ACT.Abs_reciprocal_sqrt)
 
+        cn_bank = psum.tile([P, PACK, P], F32, name="cn_bank")
+        for j in range(PACK):
+            nc.tensor.transpose(cn_bank[:, j, :], cn4[:, j : j + 1].to_broadcast([P, P]), ident[:])
+        pn4 = held.tile([P, PACK], F32, name="pn4", tag="lengths_slot")
+        nc.sync.dma_start(pn4[:], pn.rearrange("(p t) o -> p (t o)", t=PACK))
         pn1 = held.tile([P, PACK], F32, name="pn1")
         pn1_neg = held.tile([P, PACK], F32, name="pn1_neg")
         nc.gpsimd.tensor_scalar(pn1[:], pn4[:], 1.0, 1.0, ALU.mult, ALU.add)
         nc.gpsimd.tensor_scalar(pn1_neg[:], pn4[:], -1.0, -1.0, ALU.mult, ALU.add)
 
-        cn_bank = psum.tile([P, PACK, P], F32, name="cn_bank")
-        for j in range(PACK):
-            nc.tensor.transpose(cn_bank[:, j, :], cn4[:, j : j + 1].to_broadcast([P, P]), ident[:])
-        cent_raw1 = held.tile([P, PACK, HALF], F32, name="cent_raw1", tag="second_half_slot")
-        nc.sync.dma_start(cent_raw1[:], cent_rows[:, :, HALF:])
         cn_rows = held.tile([P, P, PACK], F32, name="cn_rows")
         nc.scalar.copy(out=cn_rows[:], in_=cn_bank[:].rearrange("q j p -> q p j"))
         cn_all = cn_rows[:].rearrange("q p j -> q (p j)")
 
-        got_scales = held.tile([P, I], U8, name="got_scales", align_bytes=64)
+        got_scales = held.tile([P, I], U8, name="got_scales", tag="gathered_slot", align_bytes=64)
         pt_scales = held.tile([P, PACK, P], U8, name="pt_scales", align_bytes=64)
         nc.vector.tensor_copy(got_scales[:], pool_scales[:].indirect(offsets[:]))
         nc.vector.tensor_copy(
             out=pt_scales[:].rearrange("p r (c i) -> p c r i", i=16),
             in_=got_scales[:].rearrange("p (c i r) -> p c r i", i=16, r=PACK),
         )
-        cent_words = held.tile([P, M], U32, name="cent_words", align_bytes=64)
+        cent_words = held.tile([P, M], U32, name="cent_words", tag="scales_slot", align_bytes=64)
         cent_scales = held.tile([P, M], U8, name="cent_scales", align_bytes=64)
 
         def quantise_centres(h, raw):
@@ -90,7 +92,8 @@ def tile_attend_dectarget_pl_kernel(tc, pts_words, pts_scales, cent, pn, cn, off
                 out=cent_words[:, cols].bitcast(FP8X4), scales=cent_scales[:, cols], in_=cent_bf[:].rearrange("p m j -> p (m j)")
             )
 
-        got_words = held.tile([P, I], U32, name="got_words", tag="scales_slot", align_bytes=64)
+        quantise_centres(0, cent_raw0)
+        got_words = held.tile([P, I], U32, name="got_words", tag="gathered_slot", align_bytes=64)
         pt_words = held.tile([P, PACK, P], U32, name="pt_words", align_bytes=64)
         nc.vector.tensor_copy(got_words[:], pool_words[:].indirect(offsets[:]))
         for pair in (slice(0, 2), slice(2, 4)):
@@ -98,7 +101,6 @@ def tile_attend_dectarget_pl_kernel(tc, pts_words, pts_scales, cent, pn, cn, off
                 out=pt_words[:, pair, :].bitcast(I32).rearrange("p r (c i) -> p c r i", i=4),
                 in_=got_words[:].bitcast(I32).rearrange("p (c i r) -> p c r i", i=4, r=PACK)[:, :, pair, :],
             )
-        quantise_centres(0, cent_raw0)
         quantise_centres(1, cent_raw1)
 
         def product(out, t, cols):

@@ -84,15 +84,15 @@ def tile_attend_dectarget_pl_kernel(tc, pts_words, pts_scales, cent, pn, cn, off
         cent_words = held.tile([P, M], U32, name="cent_words", tag="scales_slot", align_bytes=64)
         cent_scales = held.tile([P, M], U8, name="cent_scales", align_bytes=64)
 
-        def quantise_centres(h, raw):
+        def quantise_centres(h, raw, slot):
             cols = slice(h * HALF, (h + 1) * HALF)
-            cent_bf = held.tile([P, HALF, PACK], BF16, name="cent_bf%d" % h, align_bytes=64)
+            cent_bf = held.tile([P, HALF, PACK], BF16, name="cent_bf%d" % h, tag=slot, align_bytes=64)
             interleave(nc.scalar.copy, cent_bf[:], raw[:])
             nc.vector.quantize_mx(
                 out=cent_words[:, cols].bitcast(FP8X4), scales=cent_scales[:, cols], in_=cent_bf[:].rearrange("p m j -> p (m j)")
             )
 
-        quantise_centres(0, cent_raw0)
+        quantise_centres(0, cent_raw0, "cent_bf0")
         got_words = held.tile([P, I], U32, name="got_words", tag="gathered_slot", align_bytes=64)
         pt_words = held.tile([P, PACK, P], U32, name="pt_words", align_bytes=64)
         nc.vector.tensor_copy(got_words[:], pool_words[:].indirect(offsets[:]))
@@ -101,7 +101,7 @@ def tile_attend_dectarget_pl_kernel(tc, pts_words, pts_scales, cent, pn, cn, off
                 out=pt_words[:, pair, :].bitcast(I32).rearrange("p r (c i) -> p c r i", i=4),
                 in_=got_words[:].bitcast(I32).rearrange("p (c i r) -> p c r i", i=4, r=PACK)[:, :, pair, :],
             )
-        quantise_centres(1, cent_raw1)
+        quantise_centres(1, cent_raw1, "z0")
 
         def product(out, t, cols):
             nc.tensor.matmul_mx(
@@ -126,7 +126,7 @@ def tile_attend_dectarget_pl_kernel(tc, pts_words, pts_scales, cent, pn, cn, off
             return [held.tile([P, M], F32, name="%s%d" % (name, t)) for t in range(PACK)]
 
         def quarters(name):
-            return [held.tile([P, 2, 2, HALF], F32, name="%s%d" % (name, k)) for k in range(2)]
+            return [held.tile([P, 2, 2, HALF], F32, name="%s%d" % (name, k), tag="%s%d" % (name, k), align_bytes=64) for k in range(2)]
 
         def row(pair, t):
             return pair[0][:, :, t, :] if t < 2 else pair[1][:, t - 2, :, :]
@@ -164,10 +164,10 @@ def tile_attend_dectarget_pl_kernel(tc, pts_words, pts_scales, cent, pn, cn, off
 
         def assignments(t):
             col = slice(t, t + 1)
-            if t < PACK - 1:
+            if t < 2:
                 nc.scalar.activation(s[t][:], r[t][:], ACT.Copy, scale=r_inv[:, col])
             for j in range(PACK):
-                if t == PACK - 1 and j % 2 == 0:
+                if t >= 2 and j % 2 == 0:
                     cols = slice(j * P, (j + 2) * P)
                     nc.vector.tensor_scalar(s[t][:, cols], r[t][:, cols], r_inv[:, col], None, ALU.mult)
                 nc.tensor.matmul(
@@ -227,7 +227,8 @@ def tile_attend_dectarget_pl_kernel(tc, pts_words, pts_scales, cent, pn, cn, off
             nc.sync.dma_start(out_rows[:, t, :], y[:, t, :])
         for t in range(2, PACK):
             nc.vector.scalar_tensor_tensor(x[t][:], s2[t][:], 1.0, g_whole[:], ALU.mult, ALU.mult, accum_out=x_sum[:, t : t + 1])
-        nc.vector.reciprocal(x_inv[:, 2:4], x_sum[:, 2:4])
+        for t in range(2, PACK):
+            nc.vector.reciprocal(x_inv[:, t : t + 1], x_sum[:, t : t + 1])
         for cols in (slice(HALF, M), slice(0, HALF)):
             for t in range(2, PACK):
                 nc.vector.tensor_scalar(y[:, t, cols], x[t][:, cols], x_inv[:, t : t + 1], float(M), ALU.mult, ALU.mult)

from contextlib import ExitStack

import concourse.mybir as mybir

D, T, I, M = 512, 2048, 512, 512
FLOPS = 2 * D * I * M

F32 = mybir.dt.float32
BF16 = mybir.dt.bfloat16
I32 = mybir.dt.int32
U32 = mybir.dt.uint32
U16 = mybir.dt.uint16
U8 = mybir.dt.uint8
FP8X4 = mybir.dt.float8_e4m3fn_x4
ALU = mybir.AluOpType
ACT = mybir.ActivationFunctionType
AX = mybir.AxisListType

P = 128
PACK = 4
HALF = M // 2
HALF_BYTES = PACK * HALF * 4


def interleave(engine_copy, dst, src):
    engine_copy(out=dst.rearrange("p (c i) t -> p c t i", i=4), in_=src.rearrange("p t (c i) -> p c t i", i=4))


def tile_attend_dectarget_pl_kernel(tc, pts_words, pts_scales, cent, pn, cn, offs, out_0, out_1, out_2):
    nc = tc.nc
    with ExitStack() as ctx:
        held = ctx.enter_context(tc.tile_pool(name="held", bufs=1))
        late = ctx.enter_context(tc.tile_pool(name="late", bufs=1))
        psum = ctx.enter_context(tc.psum_pool(name="psum", bufs=1))

        offsets = held.tile([P, I // 16], U16, name="offsets")
        pool_scales = held.tile([P, T], U8, name="pool_scales", tag="scales_slot", align_bytes=64)
        cn4 = held.tile([P, PACK], F32, name="cn4", tag="lengths_slot")
        warm = held.tile([P, 1], F32, name="warm")
        warm_out = held.tile([P, 1], F32, name="warm_out")
        zeros = late.tile([P, P], F32, name="zeros", offset=HALF_BYTES - 256, align_bytes=64)
        ident = held.tile([P, P], F32, name="ident", align_bytes=64)

        nc.vector.memset(pool_scales[:].bitcast(I32), 0)
        nc.vector.memset(warm[:], 1.0)
        nc.gpsimd.memset(zeros[:], 0.0)
        nc.gpsimd.affine_select(
            out=ident[:], in_=zeros[:], pattern=[[-1, P]], compare_op=ALU.not_equal, fill=1.0, base=0, channel_multiplier=1
        )
        cent_rows = cent.rearrange("(p j) m -> p j m", j=PACK)
        cent_raw0 = held.tile([P, PACK, HALF], F32, name="cent_raw0")
        nc.sync.dma_start(offsets[:], offs)
        nc.scalar.dma_start(cn4[:], cn.rearrange("o (p j) -> p (o j)", j=PACK))
        nc.sync.dma_start(cent_raw0[:], cent_rows[:, :, :HALF])
        for q in range(4):
            nc.sync.dma_start(pool_scales[32 * q : 32 * q + 4, :].bitcast(I32), pts_scales[0, 4 * q : 4 * q + 4, :].bitcast(I32))
        pool_words = late.tile([P, T], U32, name="pool_words", offset=HALF_BYTES, align_bytes=64)
        nc.sync.dma_start(pool_words[:].bitcast(I32), pts_words[0].rearrange("p c r -> p (c r)").bitcast(I32))
        cent_raw1 = late.tile([P, PACK, HALF], F32, name="cent_raw1", offset=0, align_bytes=64)
        nc.sync.dma_start(cent_raw1[:], cent_rows[:, :, HALF:])
        nc.scalar.activation(warm_out[:], warm[:], ACT.Abs_reciprocal_sqrt)

        cn_bank = psum.tile([P, PACK, P], F32, name="cn_bank")
        for j in range(PACK):
            nc.tensor.transpose(cn_bank[:, j, :], cn4[:, j : j + 1].to_broadcast([P, P]), ident[:])
        pn4 = held.tile([P, PACK], F32, name="pn4", tag="lengths_slot")
        nc.sync.dma_start(pn4[:], pn.rearrange("(p t) o -> p (t o)", t=PACK))
        pn1 = held.tile([P, PACK], F32, name="pn1")
        pn1_neg = held.tile([P, PACK], F32, name="pn1_neg")
        nc.gpsimd.tensor_scalar(pn1[:], pn4[:], 1.0, 1.0, ALU.mult, ALU.add)
        nc.gpsimd.tensor_scalar(pn1_neg[:], pn4[:], -1.0, -1.0, ALU.mult, ALU.add)

        cn_rows = held.tile([P, P, PACK], F32, name="cn_rows")
        nc.scalar.copy(out=cn_rows[:], in_=cn_bank[:].rearrange("q j p -> q p j"))
        cn_all = cn_rows[:].rearrange("q p j -> q (p j)")

        got_scales = held.tile([P, I], U8, name="got_scales", tag="gathered_slot", align_bytes=64)
        pt_scales = held.tile([P, PACK, P], U8, name="pt_scales", align_bytes=64)
        nc.vector.tensor_copy(got_scales[:], pool_scales[:].indirect(offsets[:]))
        nc.vector.tensor_copy(
            out=pt_scales[:].rearrange("p r (c i) -> p c r i", i=16),
            in_=got_scales[:].rearrange("p (c i r) -> p c r i", i=16, r=PACK),
        )
        cent_words = held.tile([P, M], U32, name="cent_words", tag="scales_slot", align_bytes=64)
        cent_scales = held.tile([P, M], U8, name="cent_scales", align_bytes=64)

        def quantise_centres(h, raw, slot):
            cols = slice(h * HALF, (h + 1) * HALF)
            cent_bf = held.tile([P, HALF, PACK], BF16, name="cent_bf%d" % h, tag=slot, align_bytes=64)
            interleave(nc.scalar.copy, cent_bf[:], raw[:])
            nc.vector.quantize_mx(
                out=cent_words[:, cols].bitcast(FP8X4), scales=cent_scales[:, cols], in_=cent_bf[:].rearrange("p m j -> p (m j)")
            )

        quantise_centres(0, cent_raw0, "cent_bf0")
        got_words = held.tile([P, I], U32, name="got_words", tag="gathered_slot", align_bytes=64)
        pt_words = held.tile([P, PACK, P], U32, name="pt_words", align_bytes=64)
        nc.vector.tensor_copy(got_words[:], pool_words[:].indirect(offsets[:]))
        for pair in (slice(0, 2), slice(2, 4)):
            nc.vector.tensor_copy(
                out=pt_words[:, pair, :].bitcast(I32).rearrange("p r (c i) -> p c r i", i=4),
                in_=got_words[:].bitcast(I32).rearrange("p (c i r) -> p c r i", i=4, r=PACK)[:, :, pair, :],
            )
        quantise_centres(1, cent_raw1, "z0")

        def product(out, t, cols):
            nc.tensor.matmul_mx(
                out=out,
                lhsT=pt_words[:, t, :].bitcast(FP8X4),
                lhsT_scale=pt_scales[:, t, :],
                rhs=cent_words[:, cols].bitcast(FP8X4),
                rhs_scale=cent_scales[:, cols],
                start=True,
                stop=True,
            )

        a_half = [psum.tile([P, 2, HALF], F32, name="a_half%d" % h, tag="a%d" % h) for h in range(2)]
        for h in range(2):
            for t in range(2):
                product(a_half[h][:, t, :], t, slice(h * HALF, (h + 1) * HALF))
        a_whole = [psum.tile([P, M], F32, name="a_whole%d" % t) for t in range(2, PACK)]
        for t in range(2, PACK):
            product(a_whole[t - 2][:], t, slice(0, M))

        def tiles(name):
            return [held.tile([P, M], F32, name="%s%d" % (name, t)) for t in range(PACK)]

        def quarters(name):
            return [held.tile([P, 2, 2, HALF], F32, name="%s%d" % (name, k), tag="%s%d" % (name, k), align_bytes=64) for k in range(2)]

        def row(pair, t):
            return pair[0][:, :, t, :] if t < 2 else pair[1][:, t - 2, :, :]

        def halves(ap):
            return ap.rearrange("p (h c) -> p h c", h=2)

        z, u, q_abs = (quarters(n) for n in ("z", "u", "q"))
        sign, r, s, s2, x = (tiles(n) for n in ("sign", "r", "s", "s2", "x"))
        r_sum = held.tile([P, PACK], F32, name="r_sum")
        r_inv = held.tile([P, PACK], F32, name="r_inv")
        f_banks = [psum.tile([P, 2, P], F32, name="f_bank%d" % h) for h in range(2)]

        def distance_half(h):
            cn_twice = cn_all[:, h * HALF : (h + 1) * HALF].unsqueeze(1).to_broadcast([P, 2, HALF])
            nc.vector.scalar_tensor_tensor(z[0][:, h, :, :], a_half[h][:], -2.0, cn_twice, ALU.mult, ALU.add)
            for t in range(2):
                nc.scalar.activation(u[0][:, h, t, :], z[0][:, h, t, :], ACT.Abs_reciprocal_sqrt, bias=pn1[:, t : t + 1])
            nc.scalar.activation(q_abs[0][:, h, :, :], u[0][:, h, :, :], ACT.Square)

        def distance_whole(t):
            nc.vector.scalar_tensor_tensor(row(z, t), halves(a_whole[t - 2][:]), -2.0, halves(cn_all), ALU.mult, ALU.add)
            nc.scalar.activation(row(u, t), row(z, t), ACT.Abs_reciprocal_sqrt, bias=pn1[:, t : t + 1])
            nc.scalar.activation(row(q_abs, t), row(u, t), ACT.Square)

        def half_sign(t, hs):
            nc.vector.tensor_scalar(halves(sign[t][:])[:, hs, :], row(z, t)[:, hs, :], pn1_neg[:, t : t + 1], 0.5, ALU.is_ge, ALU.subtract)

        def kernel_values(t):
            col = slice(t, t + 1)
            nc.vector.scalar_tensor_tensor(
                halves(r[t][:]), row(q_abs, t), 1.0, halves(sign[t][:]), ALU.mult, ALU.mult, accum_out=r_sum[:, col]
            )
            nc.vector.reciprocal(r_inv[:, col], r_sum[:, col])

        def assignments(t):
            col = slice(t, t + 1)
            if t < 2:
                nc.scalar.activation(s[t][:], r[t][:], ACT.Copy, scale=r_inv[:, col])
            for j in range(PACK):
                if t >= 2 and j % 2 == 0:
                    cols = slice(j * P, (j + 2) * P)
                    nc.vector.tensor_scalar(s[t][:, cols], r[t][:, cols], r_inv[:, col], None, ALU.mult)
                nc.tensor.matmul(
                    f_banks[j // 2][:, j % 2, :],
                    lhsT=s[t][:, j * P : (j + 1) * P],
                    rhs=ident[:],
                    is_transpose=True,
                    start=(t == 0 and j % 2 == 0),
                    stop=(t == PACK - 1 and j % 2 == 1),
                )

        for h in range(2):
            distance_half(h)
        for t in range(2, PACK):
            distance_whole(t)
        for h in range(2):
            for t in range(2):
                half_sign(t, slice(h, h + 1))
        for t in range(PACK):
            if t >= 2:
                half_sign(t, slice(0, 2))
            kernel_values(t)
        for t in range(PACK):
            assignments(t)
        for t in range(PACK):
            nc.scalar.activation(s2[t][:], r[t][:], ACT.Square, scale=r_inv[:, t : t + 1])

        f_sum = held.tile([P, PACK], F32, name="f_sum")
        f_inv = held.tile([P, PACK], F32, name="f_inv")
        g_banks = [psum.tile([P, HALF], F32, name="g_bank%d" % h, tag="a%d" % h) for h in range(2)]
        g_whole = psum.tile([P, M], F32, name="g_whole")
        for h in range(2):
            pair = slice(2 * h, 2 * h + 2)
            nc.vector.tensor_reduce(f_sum[:, pair], f_banks[h][:], AX.X, ALU.add)
            nc.vector.reciprocal(f_inv[:, pair], f_sum[:, pair])
            for j in range(2):
                nc.tensor.transpose(g_banks[h][:, j * P : (j + 1) * P], f_inv[:, 2 * h + j : 2 * h + j + 1].to_broadcast([P, P]), ident[:])
        for j in range(PACK):
            nc.tensor.transpose(g_whole[:, j * P : (j + 1) * P], f_inv[:, j : j + 1].to_broadcast([P, P]), ident[:])

        x_part = held.tile([P, 2, 2], F32, name="x_part")
        x_sum = held.tile([P, PACK], F32, name="x_sum")
        x_inv = held.tile([P, PACK], F32, name="x_inv")
        y = held.tile([P, PACK, M], F32, name="y")
        out_rows = out_0.rearrange("(p t) m -> p t m", t=PACK)
        for h in range(2):
            cols = slice(h * HALF, (h + 1) * HALF)
            for t in range(2):
                nc.vector.scalar_tensor_tensor(
                    x[t][:, cols], s2[t][:, cols], 1.0, g_banks[h][:], ALU.mult, ALU.mult, accum_out=x_part[:, h, t : t + 1]
                )
        for t in range(2):
            col = slice(t, t + 1)
            nc.vector.tensor_scalar(x_sum[:, col], x_part[:, 0, col], x_part[:, 1, col], 1.0 / M, ALU.add, ALU.mult)
            nc.vector.reciprocal(x_inv[:, col], x_sum[:, col])
            nc.scalar.activation(y[:, t, :], x[t][:], ACT.Copy, scale=x_inv[:, col])
            nc.sync.dma_start(out_rows[:, t, :], y[:, t, :])
        for t in range(2, PACK):
            nc.vector.scalar_tensor_tensor(x[t][:], s2[t][:], 1.0, g_whole[:], ALU.mult, ALU.mult, accum_out=x_sum[:, t : t + 1])
        for t in range(2, PACK):
            nc.vector.reciprocal(x_inv[:, t : t + 1], x_sum[:, t : t + 1])
        for cols in (slice(HALF, M), slice(0, HALF)):
            for t in range(2, PACK):
                nc.vector.tensor_scalar(y[:, t, cols], x[t][:, cols], x_inv[:, t : t + 1], float(M), ALU.mult, ALU.mult)
        nc.sync.dma_start(out_rows[:, 2:4, :], y[:, 2:4, :])

        y_bf = held.tile([P, M, PACK], BF16, name="y_bf", align_bytes=64)
        y_words = held.tile([P, M], U32, name="y_words", align_bytes=64)
        y_scales = held.tile([P, M], U8, name="y_scales", align_bytes=64)
        words_out = out_1[0].rearrange("p c r -> p (c r)").bitcast(I32)
        for cols, engine_copy in ((slice(HALF, M), nc.scalar.copy), (slice(0, HALF), nc.vector.tensor_copy)):
            interleave(engine_copy, y_bf[:, cols, :], y[:, :, cols])
        for h in range(2):
            cols = slice(h * HALF, (h + 1) * HALF)
            nc.vector.quantize_mx(
                out=y_words[:, cols].bitcast(FP8X4),
                scales=y_scales[:, cols],
                in_=y_bf[:, cols, :].rearrange("p m t -> p (m t)"),
            )
            nc.sync.dma_start(words_out[:, cols], y_words[:, cols].bitcast(I32))
        for q in range(4):
            queue = nc.sync if q % 2 == 0 else nc.scalar
            queue.dma_start(out_2[0, 4 * q : 4 * q + 4, :].bitcast(I32), y_scales[32 * q : 32 * q + 4, :].bitcast(I32))
